import numpy as np
import ml_dtypes


def mxq(x, axis, fmt="e4m3"):
    dtype, down = {"e4m3": (ml_dtypes.float8_e4m3fn, 7), "e5m2": (ml_dtypes.float8_e5m2, 14)}[fmt]
    v = np.moveaxis(np.asarray(x, np.float32).astype(ml_dtypes.bfloat16).astype(np.float64), axis, -1)
    blocks = v.reshape(v.shape[:-1] + (-1, 32))
    amax = np.abs(blocks).max(-1, keepdims=True)
    byte = np.maximum(np.where(amax > 0, np.frexp(amax)[1] - 1 + 127, 0) - down, 1)
    scale = np.exp2(byte - 127.0)
    codes = (blocks / scale).astype(np.float32).astype(dtype).astype(np.float64)
    return np.moveaxis((codes * scale).reshape(v.shape), -1, axis)


WIDE = False


def mx_kscale(k):
    if not WIDE:
        return np.ones(k)
    levels = np.array([10, -10, 5, -5, 0])
    if k % 512:
        return np.exp2(np.random.permutation(np.resize(levels, k // 32))).repeat(32)
    a = np.empty((k // 512, 16))
    for p in range(k // 512):
        a[p, :8] = np.random.permutation(np.resize(levels, 8))
        for g in range(8):
            far = levels[np.abs(levels - a[p, g]) >= 10]
            a[p, g + 8] = far[np.random.randint(len(far))]
    return np.exp2(a.ravel()).repeat(32)


def f64(x):
    return np.asarray(x).astype(np.float64)


def striped(idx):
    return np.tile(idx.reshape(-1, 16).T, (8, 1)).astype(np.uint16)


def unstriped(offs):
    return offs[:16].T.reshape(-1).astype(np.int64)


def relu(v):
    return np.maximum(v, 0.0)


K, T, E, C, H, N = 1024, 768, 6, 128, 512, 384


def by_expert(wq, xq):
    return np.concatenate([wq[e].T @ xq[:, e * C:(e + 1) * C] for e in range(E)], axis=1)


def setup_inputs():
    n = np.random.standard_normal
    s = mx_kscale(K)[:, None]
    u = mx_kscale(H)
    return {
        "xT": (n((K, T)) * s).astype(np.float32),
        "w1": (n((E + 1, K, H)) / np.sqrt(K) / s[None] * u[None, None, :]).astype(np.float32),
        "w2": (n((E + 1, H, N)) / np.sqrt(H) / u[None, :, None]).astype(np.float32),
        "gate": np.tile(np.random.uniform(0.2, 1.0, E * C), (N, 1)).astype(np.float32),
        "offs": striped(np.random.permutation(T)[:E * C]),
    }


def reference(xT, w1, w2, gate, offs):
    idx = unstriped(offs)
    w1q, w2q = mxq(f64(w1), 1, "e4m3"), mxq(f64(w2), 1, "e4m3")
    xs = mxq(f64(xT), 0, "e4m3")
    hs = relu(w1q[E].T @ xs)
    ys = w2q[E].T @ mxq(hs, 0, "e4m3")
    xq = mxq(f64(xT)[:, idx], 0, "e4m3")
    h = relu(by_expert(w1q, xq))
    y = by_expert(w2q, mxq(h, 0, "e4m3"))
    out = ys
    out[:, idx] += f64(gate) * y
    return out

@@ -1,0 +1,274 @@
+from contextlib import ExitStack
+
+import concourse.mybir as mybir
+
+K, T, E, C, H, N = 1024, 768, 6, 128, 512, 384
+P = 128
+J = 4
+PASSES = K // (P * J)
+NC = N // P
+
+FLOPS = 2 * E * C * 2 * (K * H + H * N)
+BYTES = 4 * (K * T + (E + 1) * (K * H + H * N) + E * C + N * T) + 2 * E * C
+
+F32 = mybir.dt.float32
+BF16 = mybir.dt.bfloat16
+U32 = mybir.dt.uint32
+U16 = mybir.dt.uint16
+U8 = mybir.dt.uint8
+FP8X4 = mybir.dt.float8_e4m3fn_x4
+COPY = mybir.ActivationFunctionType.Copy
+RELU = mybir.ActivationFunctionType.Relu
+MULT = mybir.AluOpType.mult
+ADD = mybir.AluOpType.add
+
+RAW_BUFS = 12
+AHEAD = 10
+LAG = 2
+S1 = 112
+S2 = 84
+
+
+def tile_moe_shr_mlp_relu_kernel(tc, xT, w1, w2, gate, offs, out):
+    nc = tc.nc
+    with ExitStack() as ctx:
+        keep = ctx.enter_context(tc.tile_pool(name="keep", bufs=1))
+        rawp = ctx.enter_context(tc.tile_pool(name="rawp", bufs=RAW_BUFS))
+        once = ctx.enter_context(tc.tile_pool(name="once", bufs=1))
+        mid = ctx.enter_context(tc.tile_pool(name="mid", bufs=3))
+        gp1 = ctx.enter_context(tc.tile_pool(name="gp1", bufs=5))
+        psum = ctx.enter_context(tc.psum_pool(name="psum", bufs=4))
+
+        offsets = keep.tile([P, E * C // 16], U16)
+        gate_sb = keep.tile([P, E * C], F32)
+        x_codes = keep.tile([P, PASSES, E * C], U32, align_bytes=64)
+        x_scales = keep.tile([P, PASSES, E * C], U8, align_bytes=64)
+        ws1_codes = keep.tile([P, PASSES, H], U32, align_bytes=64)
+        ws1_scales = keep.tile([P, PASSES, H], U8, align_bytes=64)
+        ws2_codes = keep.tile([P, N], U32, align_bytes=64)
+        ws2_scales = keep.tile([P, N], U8, align_bytes=64)
+        outs = [keep.tile([P, T], F32, name=f"out{c}") for c in range(NC)]
+
+        warm = keep.tile([P, 1], F32)
+        nc.gpsimd.memset(warm[:], 0.0)
+        nc.scalar.activation(warm[:], warm[:], RELU)
+
+        items = []
+        for g in range(PASSES):
+            for u in (0, 1):
+                items.append(("x", g, u))
+        for g in range(PASSES):
+            items.append(("w1", E, g))
+        for e in range(E):
+            for g in range(PASSES):
+                items.append(("w1", e, g))
+            if e == 0:
+                items.append(("w2", E, 0))
+            items.append(("w2", e, 0))
+        raws = {}
+
+        def load(n):
+            kind, a, b = items[n]
+            raw = rawp.tile([P, J * H], F32)
+            if kind == "x":
+                rows = xT[a * 512 : (a + 1) * 512, :].rearrange("(p j) w -> p j w", j=J)
+                nc.sync.dma_start(
+                    out=raw[:, 0 : 2 * T].rearrange("p (j w) -> p j w", j=2), in_=rows[:, 2 * b : 2 * b + 2, :]
+                )
+                if n == 1:
+                    nc.sync.dma_start(offsets[:], offs)
+            elif kind == "w1":
+                nc.sync.dma_start(
+                    out=raw[:].rearrange("p (j w) -> p j w", j=J),
+                    in_=w1[a, b * 512 : (b + 1) * 512, :].rearrange("(p j) w -> p j w", j=J),
+                )
+                if a == 0 and b == 0:
+                    nc.sync.dma_start(gate_sb[:], gate[0:P, :])
+            else:
+                nc.sync.dma_start(
+                    out=raw[:, 0 : J * N].rearrange("p (j w) -> p j w", j=J),
+                    in_=w2[a, :, :].rearrange("(p j) w -> p j w", j=J),
+                )
+            raws[n] = raw
+
+        issued = [0]
+
+        def ensure(n):
+            while issued[0] < len(items) and issued[0] <= n:
+                load(issued[0])
+                issued[0] += 1
+
+        ensure(AHEAD)
+
+        def quant(codes, scales, grouped):
+            nc.vector.quantize_mx(out=codes.bitcast(FP8X4), scales=scales, in_=grouped)
+
+        for g in range(PASSES):
+            grouped_a = once.tile([P, 512 * J], BF16, align_bytes=64, name=f"grouped_a{g}")
+            grouped_b = once.tile([P, 256 * J], BF16, align_bytes=64, name=f"grouped_b{g}")
+            for u in (0, 1):
+                n = 2 * g + u
+                pairs = once.tile([P, 2 * T], BF16, align_bytes=64, name=f"pairs{n}")
+                src = raws[n][:, 0 : 2 * T].rearrange("p (e c) -> p c e", e=2)
+                dst = pairs[:].rearrange("p (c e) -> p c e", e=2)
+                if u == 0:
+                    nc.scalar.activation(dst, src, COPY)
+                else:
+                    nc.vector.tensor_copy(dst, src)
+                for grouped, a, b in ((grouped_a, 0, 32), (grouped_b, 32, 48)):
+                    words = grouped[:].bitcast(U32).rearrange("p (c u) -> p c u", u=2)
+                    nc.vector.tensor_copy(words[:, :, u], pairs[:].bitcast(U32).indirect(offsets[:, a:b]))
+            quant(x_codes[:, g, 0:512], x_scales[:, g, 0:512], grouped_a[:])
+            quant(x_codes[:, g, 512:768], x_scales[:, g, 512:768], grouped_b[:])
+
+        codes_of = {}
+
+        def interleave(n):
+            kind, e, g = items[n]
+            raw = raws[n]
+            if kind == "w1":
+                grouped = gp1.tile([P, J * H], BF16, align_bytes=64, name="w1_grouped")
+                dst = grouped[:].rearrange("p (t m j) -> p m j t", t=J, j=J)
+                src = raw[:].rearrange("p (j m t) -> p m j t", j=J, t=J)
+                split = S1
+            else:
+                grouped = mid.tile([P, J * N], BF16, align_bytes=64, name="w2_grouped")
+                dst = grouped[:].rearrange("p (c i j) -> p c j i", i=4, j=J)
+                src = raw[:, 0 : J * N].rearrange("p (j c i) -> p c j i", j=J, i=4)
+                split = S2
+            nc.scalar.activation(dst[:, :split], src[:, :split], COPY)
+            nc.vector.tensor_copy(dst[:, split:], src[:, split:])
+            return grouped
+
+        def quant_weights(n, grouped):
+            kind, e, g = items[n]
+            if kind == "w1":
+                if e == E:
+                    codes, scales = ws1_codes[:, g, :], ws1_scales[:, g, :]
+                else:
+                    w1_codes = mid.tile([P, H], U32, align_bytes=64, name=f"w1_codes{g}")
+                    w1_scales = mid.tile([P, H], U8, align_bytes=64, name=f"w1_scales{g}")
+                    codes, scales = w1_codes[:], w1_scales[:]
+                quant(codes, scales, grouped[:])
+            else:
+                if e == E:
+                    codes, scales = ws2_codes[:], ws2_scales[:]
+                else:
+                    w2_codes = mid.tile([P, N], U32, align_bytes=64)
+                    w2_scales = mid.tile([P, N], U8, align_bytes=64)
+                    codes, scales = w2_codes[:], w2_scales[:]
+                quant(codes[:, 0:256], scales[:, 0:256], grouped[:, 0:1024])
+                quant(codes[:, 256:384], scales[:, 256:384], grouped[:, 1024:1536])
+            codes_of[(kind, e, g)] = (codes, scales)
+
+        def layer1(e, s):
+            cols = slice(s * C, (s + 1) * C)
+            bank = psum.tile([P, J, C], F32, name="h_bank")
+            for t in range(J):
+                for g in range(PASSES):
+                    codes, scales = codes_of[("w1", e, g)]
+                    nc.tensor.matmul_mx(
+                        out=bank[:, t, :],
+                        lhsT=codes[:, t * P : (t + 1) * P].bitcast(FP8X4),
+                        lhsT_scale=scales[:, t * P : (t + 1) * P],
+                        rhs=x_codes[:, g, cols].bitcast(FP8X4),
+                        rhs_scale=x_scales[:, g, cols],
+                        start=(g == 0),
+                        stop=(g == PASSES - 1),
+                    )
+            return bank
+
+        def relu_h(e, bank):
+            kindname = "shared" if e == E else "routed"
+            h_grouped = mid.tile([P, C, J], BF16, align_bytes=64, name=f"h_{kindname}")
+            nc.scalar.activation(h_grouped[:], bank[:].rearrange("p t n -> p n t"), RELU)
+            return h_grouped
+
+        def quant_h(e, h_grouped):
+            kindname = "shared" if e == E else "routed"
+            h_codes = mid.tile([P, C], U32, align_bytes=64, name=f"h_codes_{kindname}")
+            h_scales = mid.tile([P, C], U8, align_bytes=64, name=f"h_scales_{kindname}")
+            quant(h_codes[:], h_scales[:], h_grouped[:].rearrange("p n j -> p (n j)"))
+            return h_codes, h_scales
+
+        def layer2(e, h):
+            h_codes, h_scales = h
+            codes, scales = codes_of[("w2", e, 0)]
+            bank = psum.tile([P, NC, C], F32, name="y_bank")
+            for c in range(NC):
+                nc.tensor.matmul_mx(
+                    out=bank[:, c, :],
+                    lhsT=codes[:, c * P : (c + 1) * P].bitcast(FP8X4),
+                    lhsT_scale=scales[:, c * P : (c + 1) * P],
+                    rhs=h_codes[:].bitcast(FP8X4),
+                    rhs_scale=h_scales[:],
+                    start=True,
+                    stop=True,
+                )
+            return bank
+
+        queue = {}
+
+        def later(n, what):
+            queue.setdefault(n, []).append(what)
+
+        state = {}
+
+        def follow_layer1(n, e, s):
+            key = (e == E, s)
+            state[key] = layer1(e, s)
+
+            def do_relu():
+                state[key] = relu_h(e, state[key])
+
+            def do_quant():
+                state[key] = quant_h(e, state[key])
+
+            later(n + 1, do_relu)
+            later(n + 2, do_quant)
+
+        def follow_layer2(n, e):
+            sb = layer2(E, state[(True, e)])
+            yb = layer2(e, state[(False, e)])
+            weighted = mid.tile([P, NC, C], F32)
+            total = mid.tile([P, NC, C], F32)
+
+            def weigh():
+                g3 = gate_sb[:, e * C : (e + 1) * C].unsqueeze(1).to_broadcast([P, NC, C])
+                nc.vector.tensor_tensor(weighted[:], yb[:], g3, MULT)
+
+            def total_up():
+                nc.vector.tensor_tensor(total[:], weighted[:], sb[:], ADD)
+
+            def scatter():
+                for c in range(NC):
+                    nc.vector.tensor_copy(outs[c][:].indirect(offsets[:, 8 * e : 8 * e + 8]), total[:, c, :])
+                    if e == E - 1:
+                        nc.sync.dma_start(out[c * P : (c + 1) * P, :], outs[c][:])
+
+            later(n + 1, weigh)
+            later(n + 2, total_up)
+            later(n + 3, scatter)
+
+        grouped_of = {}
+        for n in range(4, len(items) + 10):
+            if n < len(items):
+                ensure(n + AHEAD - 1)
+                grouped_of[n] = interleave(n)
+            for what in queue.get(n, []):
+                what()
+            q = n - LAG
+            if 4 <= q < len(items):
+                kind, e, g = items[q]
+                quant_weights(q, grouped_of[q])
+                if kind == "w1" and g == 1:
+                    if e == E:
+                        follow_layer1(n, E, 0)
+                    else:
+                        follow_layer1(n, e, e)
+                        if e + 1 < E:
+                            follow_layer1(n, E, e + 1)
+            if n - LAG - 1 >= 4 and n - LAG - 1 < len(items):
+                kind, e, g = items[n - LAG - 1]
+                if kind == "w2" and e < E:
+                    follow_layer2(n, e)

@@ -22,22 +22,20 @@ RELU = mybir.ActivationFunctionType.Relu
 MULT = mybir.AluOpType.mult
 ADD = mybir.AluOpType.add
 
-RAW_BUFS = 12
-AHEAD = 10
-LAG = 2
-S1 = 112
-S2 = 84
+RAWS = 14
+GROUPS = 6
+LAST_W1 = 44
+LAST_W2 = 32
+FIRST_X = 256
 
 
 def tile_moe_shr_mlp_relu_kernel(tc, xT, w1, w2, gate, offs, out):
     nc = tc.nc
     with ExitStack() as ctx:
         keep = ctx.enter_context(tc.tile_pool(name="keep", bufs=1))
-        rawp = ctx.enter_context(tc.tile_pool(name="rawp", bufs=RAW_BUFS))
-        once = ctx.enter_context(tc.tile_pool(name="once", bufs=1))
         mid = ctx.enter_context(tc.tile_pool(name="mid", bufs=3))
-        gp1 = ctx.enter_context(tc.tile_pool(name="gp1", bufs=5))
-        psum = ctx.enter_context(tc.psum_pool(name="psum", bufs=4))
+        psum_h = ctx.enter_context(tc.psum_pool(name="psum_h", bufs=4))
+        psum_y = ctx.enter_context(tc.psum_pool(name="psum_y", bufs=2))
 
         offsets = keep.tile([P, E * C // 16], U16)
         gate_sb = keep.tile([P, E * C], F32)
@@ -47,21 +45,19 @@ def tile_moe_shr_mlp_relu_kernel(tc, xT, w1, w2, gate, offs, out):
         ws1_scales = keep.tile([P, PASSES, H], U8, align_bytes=64)
         ws2_codes = keep.tile([P, N], U32, align_bytes=64)
         ws2_scales = keep.tile([P, N], U8, align_bytes=64)
+        hs_grouped = keep.tile([P, E * C, J], BF16, align_bytes=64)
+        hs_codes = keep.tile([P, E * C], U32, align_bytes=64)
+        hs_scales = keep.tile([P, E * C], U8, align_bytes=64)
         outs = [keep.tile([P, T], F32, name=f"out{c}") for c in range(NC)]
 
         warm = keep.tile([P, 1], F32)
         nc.gpsimd.memset(warm[:], 0.0)
         nc.scalar.activation(warm[:], warm[:], RELU)
 
-        items = []
-        for g in range(PASSES):
-            for u in (0, 1):
-                items.append(("x", g, u))
-        for g in range(PASSES):
-            items.append(("w1", E, g))
+        items = [("x", g, u) for g in range(PASSES) for u in (0, 1)]
+        items += [("w1", E, g) for g in range(PASSES)]
         for e in range(E):
-            for g in range(PASSES):
-                items.append(("w1", e, g))
+            items += [("w1", e, g) for g in range(PASSES)]
             if e == 0:
                 items.append(("w2", E, 0))
             items.append(("w2", e, 0))
@@ -69,20 +65,20 @@ def tile_moe_shr_mlp_relu_kernel(tc, xT, w1, w2, gate, offs, out):
 
         def load(n):
             kind, a, b = items[n]
-            raw = rawp.tile([P, J * H], F32)
+            raw = keep.tile([P, J * H], F32, align_bytes=64, name=f"raw{n % RAWS}")
             if kind == "x":
                 rows = xT[a * 512 : (a + 1) * 512, :].rearrange("(p j) w -> p j w", j=J)
                 nc.sync.dma_start(
                     out=raw[:, 0 : 2 * T].rearrange("p (j w) -> p j w", j=2), in_=rows[:, 2 * b : 2 * b + 2, :]
                 )
-                if n == 1:
+                if n == 0:
                     nc.sync.dma_start(offsets[:], offs)
             elif kind == "w1":
                 nc.sync.dma_start(
                     out=raw[:].rearrange("p (j w) -> p j w", j=J),
                     in_=w1[a, b * 512 : (b + 1) * 512, :].rearrange("(p j) w -> p j w", j=J),
                 )
-                if a == 0 and b == 0:
+                if a == 0 and b == 1:
                     nc.sync.dma_start(gate_sb[:], gate[0:P, :])
             else:
                 nc.sync.dma_start(
@@ -91,57 +87,62 @@ def tile_moe_shr_mlp_relu_kernel(tc, xT, w1, w2, gate, offs, out):
                 )
             raws[n] = raw
 
-        issued = [0]
+        loaded = set()
 
-        def ensure(n):
-            while issued[0] < len(items) and issued[0] <= n:
-                load(issued[0])
-                issued[0] += 1
+        def load_up_to(n):
+            for m in range(min(n + 1, len(items))):
+                if m not in loaded:
+                    load(m)
+                    loaded.add(m)
 
-        ensure(AHEAD)
+        load_up_to(RAWS - 1)
 
         def quant(codes, scales, grouped):
             nc.vector.quantize_mx(out=codes.bitcast(FP8X4), scales=scales, in_=grouped)
 
         for g in range(PASSES):
-            grouped_a = once.tile([P, 512 * J], BF16, align_bytes=64, name=f"grouped_a{g}")
-            grouped_b = once.tile([P, 256 * J], BF16, align_bytes=64, name=f"grouped_b{g}")
+            grouped_a = keep.tile([P, 512 * J], BF16, align_bytes=64, name=f"grouped_a{g}")
+            grouped_b = keep.tile([P, 256 * J], BF16, align_bytes=64, name=f"grouped_b{g}")
             for u in (0, 1):
                 n = 2 * g + u
-                pairs = once.tile([P, 2 * T], BF16, align_bytes=64, name=f"pairs{n}")
+                pairs = keep.tile([P, 2 * T], BF16, align_bytes=64, name=f"pairs{n}")
                 src = raws[n][:, 0 : 2 * T].rearrange("p (e c) -> p c e", e=2)
                 dst = pairs[:].rearrange("p (c e) -> p c e", e=2)
-                if u == 0:
-                    nc.scalar.activation(dst, src, COPY)
+                if n == 0:
+                    nc.scalar.activation(dst[:, :FIRST_X], src[:, :FIRST_X], COPY)
+                    nc.vector.tensor_copy(dst[:, FIRST_X:], src[:, FIRST_X:])
                 else:
-                    nc.vector.tensor_copy(dst, src)
+                    nc.scalar.activation(dst, src, COPY)
                 for grouped, a, b in ((grouped_a, 0, 32), (grouped_b, 32, 48)):
                     words = grouped[:].bitcast(U32).rearrange("p (c u) -> p c u", u=2)
                     nc.vector.tensor_copy(words[:, :, u], pairs[:].bitcast(U32).indirect(offsets[:, a:b]))
             quant(x_codes[:, g, 0:512], x_scales[:, g, 0:512], grouped_a[:])
             quant(x_codes[:, g, 512:768], x_scales[:, g, 512:768], grouped_b[:])
 
+        grouped_of = {}
         codes_of = {}
 
         def interleave(n):
             kind, e, g = items[n]
             raw = raws[n]
+            grouped = keep.tile([P, J * H], BF16, align_bytes=64, name=f"grouped{n % GROUPS}")
             if kind == "w1":
-                grouped = gp1.tile([P, J * H], BF16, align_bytes=64, name="w1_grouped")
                 dst = grouped[:].rearrange("p (t m j) -> p m j t", t=J, j=J)
                 src = raw[:].rearrange("p (j m t) -> p m j t", j=J, t=J)
-                split = S1
+                split = LAST_W1 if n == len(items) - 2 else P
             else:
-                grouped = mid.tile([P, J * N], BF16, align_bytes=64, name="w2_grouped")
-                dst = grouped[:].rearrange("p (c i j) -> p c j i", i=4, j=J)
+                dst = grouped[:, 0 : J * N].rearrange("p (c i j) -> p c j i", i=4, j=J)
                 src = raw[:, 0 : J * N].rearrange("p (j c i) -> p c j i", j=J, i=4)
-                split = S2
-            nc.scalar.activation(dst[:, :split], src[:, :split], COPY)
-            nc.vector.tensor_copy(dst[:, split:], src[:, split:])
-            return grouped
+                split = LAST_W2 if n == len(items) - 1 else 0
+            if split > 0:
+                nc.scalar.activation(dst[:, :split], src[:, :split], COPY)
+            if split < dst.shape[1]:
+                nc.vector.tensor_copy(dst[:, split:], src[:, split:])
+            grouped_of[n] = grouped
 
-        def quant_weights(n, grouped):
+        def quant_weights(n):
             kind, e, g = items[n]
+            grouped = grouped_of[n]
             if kind == "w1":
                 if e == E:
                     codes, scales = ws1_codes[:, g, :], ws1_scales[:, g, :]
@@ -163,7 +164,7 @@ def tile_moe_shr_mlp_relu_kernel(tc, xT, w1, w2, gate, offs, out):
 
         def layer1(e, s):
             cols = slice(s * C, (s + 1) * C)
-            bank = psum.tile([P, J, C], F32, name="h_bank")
+            bank = psum_h.tile([P, J, C], F32, name="h_bank")
             for t in range(J):
                 for g in range(PASSES):
                     codes, scales = codes_of[("w1", e, g)]
@@ -178,97 +179,89 @@ def tile_moe_shr_mlp_relu_kernel(tc, xT, w1, w2, gate, offs, out):
                     )
             return bank
 
-        def relu_h(e, bank):
-            kindname = "shared" if e == E else "routed"
-            h_grouped = mid.tile([P, C, J], BF16, align_bytes=64, name=f"h_{kindname}")
-            nc.scalar.activation(h_grouped[:], bank[:].rearrange("p t n -> p n t"), RELU)
-            return h_grouped
+        def relu(dst, bank):
+            nc.scalar.activation(dst, bank[:].rearrange("p t n -> p n t"), RELU)
 
-        def quant_h(e, h_grouped):
-            kindname = "shared" if e == E else "routed"
-            h_codes = mid.tile([P, C], U32, align_bytes=64, name=f"h_codes_{kindname}")
-            h_scales = mid.tile([P, C], U8, align_bytes=64, name=f"h_scales_{kindname}")
-            quant(h_codes[:], h_scales[:], h_grouped[:].rearrange("p n j -> p (n j)"))
-            return h_codes, h_scales
-
-        def layer2(e, h):
-            h_codes, h_scales = h
+        def layer2(e, h_codes, h_scales, name):
             codes, scales = codes_of[("w2", e, 0)]
-            bank = psum.tile([P, NC, C], F32, name="y_bank")
+            bank = psum_y.tile([P, NC, C], F32, name=name)
             for c in range(NC):
                 nc.tensor.matmul_mx(
                     out=bank[:, c, :],
                     lhsT=codes[:, c * P : (c + 1) * P].bitcast(FP8X4),
                     lhsT_scale=scales[:, c * P : (c + 1) * P],
-                    rhs=h_codes[:].bitcast(FP8X4),
-                    rhs_scale=h_scales[:],
+                    rhs=h_codes.bitcast(FP8X4),
+                    rhs_scale=h_scales,
                     start=True,
                     stop=True,
                 )
             return bank
 
-        queue = {}
+        h_banks = {}
+        h_tiles = {}
+        y_banks = {}
+        sums = {}
 
-        def later(n, what):
-            queue.setdefault(n, []).append(what)
+        def shared_hidden():
+            for s in range(E):
+                relu(hs_grouped[:, s * C : (s + 1) * C, :], layer1(E, s))
+            flat = hs_grouped[:].rearrange("p n j -> p (n j)")
+            quant(hs_codes[:, 0:512], hs_scales[:, 0:512], flat[:, 0:2048])
+            quant(hs_codes[:, 512:768], hs_scales[:, 512:768], flat[:, 2048:3072])
 
-        state = {}
+        def hidden(e, name):
+            h_grouped = keep.tile([P, C * J], BF16, align_bytes=64, name=name)
+            relu(h_grouped[:].rearrange("p (n j) -> p n j", j=J), h_banks[e])
+            h_tiles[e] = h_grouped
 
-        def follow_layer1(n, e, s):
-            key = (e == E, s)
-            state[key] = layer1(e, s)
+        def outputs(e):
+            h_codes = mid.tile([P, C], U32, align_bytes=64)
+            h_scales = mid.tile([P, C], U8, align_bytes=64)
+            quant(h_codes[:], h_scales[:], h_tiles[e][:])
+            cols = slice(e * C, (e + 1) * C)
+            ys = layer2(E, hs_codes[:, cols], hs_scales[:, cols], "ys_bank")
+            y_banks[e] = (layer2(e, h_codes[:], h_scales[:], "y_bank"), ys)
 
-            def do_relu():
-                state[key] = relu_h(e, state[key])
+        def weigh(e, name):
+            weighted = keep.tile([P, NC, C], F32, align_bytes=64, name=name)
+            g3 = gate_sb[:, e * C : (e + 1) * C].unsqueeze(1).to_broadcast([P, NC, C])
+            nc.vector.tensor_tensor(weighted[:], y_banks[e][0][:], g3, MULT)
+            sums[e] = weighted
 
-            def do_quant():
-                state[key] = quant_h(e, state[key])
+        def add_and_scatter(e, name):
+            total = keep.tile([P, NC, C], F32, align_bytes=64, name=name)
+            nc.vector.tensor_tensor(total[:], sums[e][:], y_banks[e][1][:], ADD)
+            for c in range(NC):
+                nc.vector.tensor_copy(outs[c][:].indirect(offsets[:, 8 * e : 8 * e + 8]), total[:, c, :])
+                if e == E - 1:
+                    nc.sync.dma_start(out[c * P : (c + 1) * P, :], outs[c][:])
 
-            later(n + 1, do_relu)
-            later(n + 2, do_quant)
-
-        def follow_layer2(n, e):
-            sb = layer2(E, state[(True, e)])
-            yb = layer2(e, state[(False, e)])
-            weighted = mid.tile([P, NC, C], F32)
-            total = mid.tile([P, NC, C], F32)
-
-            def weigh():
-                g3 = gate_sb[:, e * C : (e + 1) * C].unsqueeze(1).to_broadcast([P, NC, C])
-                nc.vector.tensor_tensor(weighted[:], yb[:], g3, MULT)
-
-            def total_up():
-                nc.vector.tensor_tensor(total[:], weighted[:], sb[:], ADD)
-
-            def scatter():
-                for c in range(NC):
-                    nc.vector.tensor_copy(outs[c][:].indirect(offsets[:, 8 * e : 8 * e + 8]), total[:, c, :])
-                    if e == E - 1:
-                        nc.sync.dma_start(out[c * P : (c + 1) * P, :], outs[c][:])
-
-            later(n + 1, weigh)
-            later(n + 2, total_up)
-            later(n + 3, scatter)
-
-        grouped_of = {}
-        for n in range(4, len(items) + 10):
-            if n < len(items):
-                ensure(n + AHEAD - 1)
-                grouped_of[n] = interleave(n)
-            for what in queue.get(n, []):
-                what()
-            q = n - LAG
-            if 4 <= q < len(items):
-                kind, e, g = items[q]
-                quant_weights(q, grouped_of[q])
-                if kind == "w1" and g == 1:
-                    if e == E:
-                        follow_layer1(n, E, 0)
-                    else:
-                        follow_layer1(n, e, e)
-                        if e + 1 < E:
-                            follow_layer1(n, E, e + 1)
-            if n - LAG - 1 >= 4 and n - LAG - 1 < len(items):
-                kind, e, g = items[n - LAG - 1]
-                if kind == "w2" and e < E:
-                    follow_layer2(n, e)
+        for n in range(4, len(items)):
+            kind, e, g = items[n]
+            load_up_to(n + RAWS - 5)
+            interleave(n)
+            if kind == "w1" and g == 0 and 1 <= e < E:
+                hidden(e - 1, f"raw{n % RAWS}")
+            if n > 4:
+                quant_weights(n - 1)
+            if kind == "w1" and g == 0 and e == 0:
+                shared_hidden()
+            if kind == "w1" and g == 0 and 2 <= e < E:
+                add_and_scatter(e - 2, f"grouped{(n - 1) % GROUPS}")
+            if kind == "w1" and g == 1 and 1 <= e < E:
+                outputs(e - 1)
+                if e == E - 1:
+                    weigh(e - 1, f"grouped{(n - 1) % GROUPS}")
+            if kind == "w2" and items[n - 1][0] == "w1":
+                r = items[n - 1][1]
+                h_banks[r] = layer1(r, r)
+                if 1 <= r < E - 1:
+                    weigh(r - 1, f"grouped{(n - 1) % GROUPS}")
+                if r == E - 1:
+                    add_and_scatter(r - 1, f"grouped{(n - 1) % GROUPS}")
+        last = E - 1
+        hidden(last, "h_last")
+        quant_weights(len(items) - 1)
+        outputs(last)
+        weigh(last, "weighted_last")
+        add_and_scatter(last, "total_last")

@@ -25,7 +25,8 @@ ADD = mybir.AluOpType.add
 RAWS = 14
 GROUPS = 6
 LAST_W1 = 44
-LAST_W2 = 32
+W2_SCALAR = (0, 0, 0, 0, 0, 24, 0)
+W2_GPSIMD = (96, 96, 96, 96, 96, 24, 96)
 FIRST_X = 256
 
 
@@ -133,11 +134,17 @@ def tile_moe_shr_mlp_relu_kernel(tc, xT, w1, w2, gate, offs, out):
             else:
                 dst = grouped[:, 0 : J * N].rearrange("p (c i j) -> p c j i", i=4, j=J)
                 src = raw[:, 0 : J * N].rearrange("p (j c i) -> p c j i", j=J, i=4)
-                split = LAST_W2 if n == len(items) - 1 else 0
+                split = W2_SCALAR[e]
+                if W2_GPSIMD[e] > 0:
+                    a = 4 * (96 - W2_GPSIMD[e])
+                    dst_n = grouped[:, 0 : J * N].rearrange("p (n j) -> p n j", j=J)
+                    src_n = raw[:, 0 : J * N].rearrange("p (j n) -> p n j", j=J)
+                    nc.gpsimd.tensor_scalar(dst_n[:, a:], src_n[:, a:], 1.0, 0.0, MULT, ADD)
             if split > 0:
                 nc.scalar.activation(dst[:, :split], src[:, :split], COPY)
-            if split < dst.shape[1]:
-                nc.vector.tensor_copy(dst[:, split:], src[:, split:])
+            rest = dst.shape[1] - (W2_GPSIMD[e] if kind == "w2" else 0)
+            if split < rest:
+                nc.vector.tensor_copy(dst[:, split:rest], src[:, split:rest])
             grouped_of[n] = grouped
 
         def quant_weights(n):
@@ -230,7 +237,8 @@ def tile_moe_shr_mlp_relu_kernel(tc, xT, w1, w2, gate, offs, out):
 
         def add_and_scatter(e, name):
             total = keep.tile([P, NC, C], F32, align_bytes=64, name=name)
-            nc.vector.tensor_tensor(total[:], sums[e][:], y_banks[e][1][:], ADD)
+            for c in range(NC):
+                nc.vector.tensor_tensor(total[:, c, :], sums[e][:, c, :], y_banks[e][1][:, c, :], ADD)
             for c in range(NC):
                 nc.vector.tensor_copy(outs[c][:].indirect(offsets[:, 8 * e : 8 * e + 8]), total[:, c, :])
                 if e == E - 1:

from contextlib import ExitStack

import concourse.mybir as mybir

K, T, E, C, H, N = 1024, 768, 6, 128, 512, 384
P = 128
J = 4
PASSES = K // (P * J)
NC = N // P

FLOPS = 2 * E * C * 2 * (K * H + H * N)
BYTES = 4 * (K * T + (E + 1) * (K * H + H * N) + E * C + N * T) + 2 * E * C

F32 = mybir.dt.float32
BF16 = mybir.dt.bfloat16
U32 = mybir.dt.uint32
U16 = mybir.dt.uint16
U8 = mybir.dt.uint8
FP8X4 = mybir.dt.float8_e4m3fn_x4
COPY = mybir.ActivationFunctionType.Copy
RELU = mybir.ActivationFunctionType.Relu
MULT = mybir.AluOpType.mult
ADD = mybir.AluOpType.add

RAWS = 14
GROUPS = 6
LAST_W1 = 44
W2_SCALAR = (0, 0, 0, 0, 0, 24, 0)
W2_GPSIMD = (96, 96, 96, 96, 96, 24, 96)
FIRST_X = 256


def tile_moe_shr_mlp_relu_kernel(tc, xT, w1, w2, gate, offs, out):
    nc = tc.nc
    with ExitStack() as ctx:
        keep = ctx.enter_context(tc.tile_pool(name="keep", bufs=1))
        mid = ctx.enter_context(tc.tile_pool(name="mid", bufs=3))
        psum_h = ctx.enter_context(tc.psum_pool(name="psum_h", bufs=4))
        psum_y = ctx.enter_context(tc.psum_pool(name="psum_y", bufs=2))

        offsets = keep.tile([P, E * C // 16], U16)
        gate_sb = keep.tile([P, E * C], F32)
        x_codes = keep.tile([P, PASSES, E * C], U32, align_bytes=64)
        x_scales = keep.tile([P, PASSES, E * C], U8, align_bytes=64)
        ws1_codes = keep.tile([P, PASSES, H], U32, align_bytes=64)
        ws1_scales = keep.tile([P, PASSES, H], U8, align_bytes=64)
        ws2_codes = keep.tile([P, N], U32, align_bytes=64)
        ws2_scales = keep.tile([P, N], U8, align_bytes=64)
        hs_grouped = keep.tile([P, E * C, J], BF16, align_bytes=64)
        hs_codes = keep.tile([P, E * C], U32, align_bytes=64)
        hs_scales = keep.tile([P, E * C], U8, align_bytes=64)
        outs = [keep.tile([P, T], F32, name=f"out{c}") for c in range(NC)]

        warm = keep.tile([P, 1], F32)
        nc.gpsimd.memset(warm[:], 0.0)
        nc.scalar.activation(warm[:], warm[:], RELU)

        items = [("x", g, u) for g in range(PASSES) for u in (0, 1)]
        items += [("w1", E, g) for g in range(PASSES)]
        for e in range(E):
            items += [("w1", e, g) for g in range(PASSES)]
            if e == 0:
                items.append(("w2", E, 0))
            items.append(("w2", e, 0))
        raws = {}

        def load(n):
            kind, a, b = items[n]
            raw = keep.tile([P, J * H], F32, align_bytes=64, name=f"raw{n % RAWS}")
            if kind == "x":
                rows = xT[a * 512 : (a + 1) * 512, :].rearrange("(p j) w -> p j w", j=J)
                nc.sync.dma_start(
                    out=raw[:, 0 : 2 * T].rearrange("p (j w) -> p j w", j=2), in_=rows[:, 2 * b : 2 * b + 2, :]
                )
                if n == 0:
                    nc.sync.dma_start(offsets[:], offs)
            elif kind == "w1":
                nc.sync.dma_start(
                    out=raw[:].rearrange("p (j w) -> p j w", j=J),
                    in_=w1[a, b * 512 : (b + 1) * 512, :].rearrange("(p j) w -> p j w", j=J),
                )
                if a == 0 and b == 1:
                    nc.sync.dma_start(gate_sb[:], gate[0:P, :])
            else:
                nc.sync.dma_start(
                    out=raw[:, 0 : J * N].rearrange("p (j w) -> p j w", j=J),
                    in_=w2[a, :, :].rearrange("(p j) w -> p j w", j=J),
                )
            raws[n] = raw

        loaded = set()

        def load_up_to(n):
            for m in range(min(n + 1, len(items))):
                if m not in loaded:
                    load(m)
                    loaded.add(m)

        load_up_to(RAWS - 1)

        def quant(codes, scales, grouped):
            nc.vector.quantize_mx(out=codes.bitcast(FP8X4), scales=scales, in_=grouped)

        for g in range(PASSES):
            grouped_a = keep.tile([P, 512 * J], BF16, align_bytes=64, name=f"grouped_a{g}")
            grouped_b = keep.tile([P, 256 * J], BF16, align_bytes=64, name=f"grouped_b{g}")
            for u in (0, 1):
                n = 2 * g + u
                pairs = keep.tile([P, 2 * T], BF16, align_bytes=64, name=f"pairs{n}")
                src = raws[n][:, 0 : 2 * T].rearrange("p (e c) -> p c e", e=2)
                dst = pairs[:].rearrange("p (c e) -> p c e", e=2)
                if n == 0:
                    nc.scalar.activation(dst[:, :FIRST_X], src[:, :FIRST_X], COPY)
                    nc.vector.tensor_copy(dst[:, FIRST_X:], src[:, FIRST_X:])
                else:
                    nc.scalar.activation(dst, src, COPY)
                for grouped, a, b in ((grouped_a, 0, 32), (grouped_b, 32, 48)):
                    words = grouped[:].bitcast(U32).rearrange("p (c u) -> p c u", u=2)
                    nc.vector.tensor_copy(words[:, :, u], pairs[:].bitcast(U32).indirect(offsets[:, a:b]))
            quant(x_codes[:, g, 0:512], x_scales[:, g, 0:512], grouped_a[:])
            quant(x_codes[:, g, 512:768], x_scales[:, g, 512:768], grouped_b[:])

        grouped_of = {}
        codes_of = {}

        def interleave(n):
            kind, e, g = items[n]
            raw = raws[n]
            grouped = keep.tile([P, J * H], BF16, align_bytes=64, name=f"grouped{n % GROUPS}")
            if kind == "w1":
                dst = grouped[:].rearrange("p (t m j) -> p m j t", t=J, j=J)
                src = raw[:].rearrange("p (j m t) -> p m j t", j=J, t=J)
                split = LAST_W1 if n == len(items) - 2 else P
            else:
                dst = grouped[:, 0 : J * N].rearrange("p (c i j) -> p c j i", i=4, j=J)
                src = raw[:, 0 : J * N].rearrange("p (j c i) -> p c j i", j=J, i=4)
                split = W2_SCALAR[e]
                if W2_GPSIMD[e] > 0:
                    a = 4 * (96 - W2_GPSIMD[e])
                    dst_n = grouped[:, 0 : J * N].rearrange("p (n j) -> p n j", j=J)
                    src_n = raw[:, 0 : J * N].rearrange("p (j n) -> p n j", j=J)
                    nc.gpsimd.tensor_scalar(dst_n[:, a:], src_n[:, a:], 1.0, 0.0, MULT, ADD)
            if split > 0:
                nc.scalar.activation(dst[:, :split], src[:, :split], COPY)
            rest = dst.shape[1] - (W2_GPSIMD[e] if kind == "w2" else 0)
            if split < rest:
                nc.vector.tensor_copy(dst[:, split:rest], src[:, split:rest])
            grouped_of[n] = grouped

        def quant_weights(n):
            kind, e, g = items[n]
            grouped = grouped_of[n]
            if kind == "w1":
                if e == E:
                    codes, scales = ws1_codes[:, g, :], ws1_scales[:, g, :]
                else:
                    w1_codes = mid.tile([P, H], U32, align_bytes=64, name=f"w1_codes{g}")
                    w1_scales = mid.tile([P, H], U8, align_bytes=64, name=f"w1_scales{g}")
                    codes, scales = w1_codes[:], w1_scales[:]
                quant(codes, scales, grouped[:])
            else:
                if e == E:
                    codes, scales = ws2_codes[:], ws2_scales[:]
                else:
                    w2_codes = mid.tile([P, N], U32, align_bytes=64)
                    w2_scales = mid.tile([P, N], U8, align_bytes=64)
                    codes, scales = w2_codes[:], w2_scales[:]
                quant(codes[:, 0:256], scales[:, 0:256], grouped[:, 0:1024])
                quant(codes[:, 256:384], scales[:, 256:384], grouped[:, 1024:1536])
            codes_of[(kind, e, g)] = (codes, scales)

        def layer1(e, s):
            cols = slice(s * C, (s + 1) * C)
            bank = psum_h.tile([P, J, C], F32, name="h_bank")
            for t in range(J):
                for g in range(PASSES):
                    codes, scales = codes_of[("w1", e, g)]
                    nc.tensor.matmul_mx(
                        out=bank[:, t, :],
                        lhsT=codes[:, t * P : (t + 1) * P].bitcast(FP8X4),
                        lhsT_scale=scales[:, t * P : (t + 1) * P],
                        rhs=x_codes[:, g, cols].bitcast(FP8X4),
                        rhs_scale=x_scales[:, g, cols],
                        start=(g == 0),
                        stop=(g == PASSES - 1),
                    )
            return bank

        def relu(dst, bank):
            nc.scalar.activation(dst, bank[:].rearrange("p t n -> p n t"), RELU)

        def layer2(e, h_codes, h_scales, name):
            codes, scales = codes_of[("w2", e, 0)]
            bank = psum_y.tile([P, NC, C], F32, name=name)
            for c in range(NC):
                nc.tensor.matmul_mx(
                    out=bank[:, c, :],
                    lhsT=codes[:, c * P : (c + 1) * P].bitcast(FP8X4),
                    lhsT_scale=scales[:, c * P : (c + 1) * P],
                    rhs=h_codes.bitcast(FP8X4),
                    rhs_scale=h_scales,
                    start=True,
                    stop=True,
                )
            return bank

        h_banks = {}
        h_tiles = {}
        y_banks = {}
        sums = {}

        def shared_hidden():
            for s in range(E):
                relu(hs_grouped[:, s * C : (s + 1) * C, :], layer1(E, s))
            flat = hs_grouped[:].rearrange("p n j -> p (n j)")
            quant(hs_codes[:, 0:512], hs_scales[:, 0:512], flat[:, 0:2048])
            quant(hs_codes[:, 512:768], hs_scales[:, 512:768], flat[:, 2048:3072])

        def hidden(e, name):
            h_grouped = keep.tile([P, C * J], BF16, align_bytes=64, name=name)
            relu(h_grouped[:].rearrange("p (n j) -> p n j", j=J), h_banks[e])
            h_tiles[e] = h_grouped

        def outputs(e):
            h_codes = mid.tile([P, C], U32, align_bytes=64)
            h_scales = mid.tile([P, C], U8, align_bytes=64)
            quant(h_codes[:], h_scales[:], h_tiles[e][:])
            cols = slice(e * C, (e + 1) * C)
            ys = layer2(E, hs_codes[:, cols], hs_scales[:, cols], "ys_bank")
            y_banks[e] = (layer2(e, h_codes[:], h_scales[:], "y_bank"), ys)

        def weigh(e, name):
            weighted = keep.tile([P, NC, C], F32, align_bytes=64, name=name)
            g3 = gate_sb[:, e * C : (e + 1) * C].unsqueeze(1).to_broadcast([P, NC, C])
            nc.vector.tensor_tensor(weighted[:], y_banks[e][0][:], g3, MULT)
            sums[e] = weighted

        def add_and_scatter(e, name):
            total = keep.tile([P, NC, C], F32, align_bytes=64, name=name)
            for c in range(NC):
                nc.vector.tensor_tensor(total[:, c, :], sums[e][:, c, :], y_banks[e][1][:, c, :], ADD)
            for c in range(NC):
                nc.vector.tensor_copy(outs[c][:].indirect(offsets[:, 8 * e : 8 * e + 8]), total[:, c, :])
                if e == E - 1:
                    nc.sync.dma_start(out[c * P : (c + 1) * P, :], outs[c][:])

        for n in range(4, len(items)):
            kind, e, g = items[n]
            load_up_to(n + RAWS - 5)
            interleave(n)
            if kind == "w1" and g == 0 and 1 <= e < E:
                hidden(e - 1, f"raw{n % RAWS}")
            if n > 4:
                quant_weights(n - 1)
            if kind == "w1" and g == 0 and e == 0:
                shared_hidden()
            if kind == "w1" and g == 0 and 2 <= e < E:
                add_and_scatter(e - 2, f"grouped{(n - 1) % GROUPS}")
            if kind == "w1" and g == 1 and 1 <= e < E:
                outputs(e - 1)
                if e == E - 1:
                    weigh(e - 1, f"grouped{(n - 1) % GROUPS}")
            if kind == "w2" and items[n - 1][0] == "w1":
                r = items[n - 1][1]
                h_banks[r] = layer1(r, r)
                if 1 <= r < E - 1:
                    weigh(r - 1, f"grouped{(n - 1) % GROUPS}")
                if r == E - 1:
                    add_and_scatter(r - 1, f"grouped{(n - 1) % GROUPS}")
        last = E - 1
        hidden(last, "h_last")
        quant_weights(len(items) - 1)
        outputs(last)
        weigh(last, "weighted_last")
        add_and_scatter(last, "total_last")
